import numpy as np
import ml_dtypes


def mxq(x, axis, fmt="e4m3"):
    dtype, down = {"e4m3": (ml_dtypes.float8_e4m3fn, 7), "e5m2": (ml_dtypes.float8_e5m2, 14)}[fmt]
    v = np.moveaxis(np.asarray(x, np.float32).astype(ml_dtypes.bfloat16).astype(np.float64), axis, -1)
    blocks = v.reshape(v.shape[:-1] + (-1, 32))
    amax = np.abs(blocks).max(-1, keepdims=True)
    byte = np.maximum(np.where(amax > 0, np.frexp(amax)[1] - 1 + 127, 0) - down, 1)
    scale = np.exp2(byte - 127.0)
    codes = (blocks / scale).astype(np.float32).astype(dtype).astype(np.float64)
    return np.moveaxis((codes * scale).reshape(v.shape), -1, axis)


WIDE = False


def mx_kscale(k):
    if not WIDE:
        return np.ones(k)
    levels = np.array([10, -10, 5, -5, 0])
    if k % 512:
        return np.exp2(np.random.permutation(np.resize(levels, k // 32))).repeat(32)
    a = np.empty((k // 512, 16))
    for p in range(k // 512):
        a[p, :8] = np.random.permutation(np.resize(levels, 8))
        for g in range(8):
            far = levels[np.abs(levels - a[p, g]) >= 10]
            a[p, g + 8] = far[np.random.randint(len(far))]
    return np.exp2(a.ravel()).repeat(32)


def f64(x):
    return np.asarray(x).astype(np.float64)


def striped(idx):
    return np.tile(idx.reshape(-1, 16).T, (8, 1)).astype(np.uint16)


def unstriped(offs):
    return offs[:16].T.reshape(-1).astype(np.int64)


K, T, E, C, N = 512, 512, 4, 256, 1536


def by_expert(wq, xq):
    return np.concatenate([wq[e].T @ xq[:, e * C:(e + 1) * C] for e in range(E)], axis=1)


def setup_inputs():
    n = np.random.standard_normal
    s = mx_kscale(N)[:, None]
    first = np.random.permutation(np.repeat(np.arange(E), T // E))
    second = (first + 1 + np.random.permutation(np.repeat(np.arange(E - 1), -(-T // (E - 1)))[:T])) % E
    while np.bincount(second, minlength=E).max() != T // E:
        load = np.bincount(second, minlength=E); hi, lo = int(load.argmax()), int(load.argmin())
        t = np.flatnonzero((second == hi) & (first != lo))[0]; second[t] = lo
    slot_token = np.empty(E * C, np.int64); pos = np.empty((2, T), np.int64); fill = np.zeros(E, np.int64)
    place = np.stack([np.random.permutation(C) for _ in range(E)])
    for r, deal in enumerate((first, second)):
        for t in np.random.permutation(T):
            e = deal[t]; j = e * C + place[e, fill[e]]; fill[e] += 1; slot_token[j] = t; pos[r, t] = j
    g = np.random.uniform(0.2, 0.8, T)
    w_slot = np.empty(E * C); w_slot[pos[0]] = g; w_slot[pos[1]] = 1.0 - g
    return {
        "dyT": (n((N, T)) * s).astype(np.float32),
        "w": (n((E, N, K)) / np.sqrt(N) / s[None]).astype(np.float32),
        "gate": np.tile(w_slot, (N, 1)).astype(np.float32),
        "offs": striped(slot_token),
        "pos1": striped(pos[0]),
        "pos2": striped(pos[1]),
    }


def reference(dyT, w, gate, offs, pos1, pos2):
    idx = unstriped(offs)
    gq = mxq(f64(gate) * f64(dyT)[:, idx], 0, "e4m3")
    dx = by_expert(mxq(f64(w), 1, "e4m3"), gq)
    return dx[:, unstriped(pos1)] + dx[:, unstriped(pos2)]

@@ -1,0 +1,170 @@
+from contextlib import ExitStack
+
+import concourse.mybir as mybir
+
+K, T, E, C, N = 512, 512, 4, 256, 1536
+S = E * C
+P = 128
+PACK = 4
+PASS = P * PACK
+NPASS = N // PASS
+HALF = 512
+WIN = T + 8
+COLS = 256
+
+F32 = mybir.dt.float32
+BF16 = mybir.dt.bfloat16
+U32 = mybir.dt.uint32
+U16 = mybir.dt.uint16
+U8 = mybir.dt.uint8
+FP8X4 = mybir.dt.float8_e4m3fn_x4
+ADD = mybir.AluOpType.add
+MULT = mybir.AluOpType.mult
+
+FLOPS = 2 * K * N * S
+BYTES = 4 * (N * T + E * N * K + S + K * T) + 2 * 128 * (64 + 32 + 32)
+
+VECTOR_B = (10, 11)
+
+
+def tile_moe_bdx_lin_none_kernel(tc, dyT, w, gate, offs, pos1, pos2, out):
+    nc = tc.nc
+    with ExitStack() as ctx:
+        held = ctx.enter_context(tc.tile_pool(name="held", bufs=1))
+        wraws = ctx.enter_context(tc.tile_pool(name="wraws", bufs=12))
+        wbfs = ctx.enter_context(tc.tile_pool(name="wbfs", bufs=12))
+        gs = ctx.enter_context(tc.tile_pool(name="gs", bufs=2))
+        psum = ctx.enter_context(tc.psum_pool(name="psum", bufs=8))
+
+        offs_sb = held.tile([P, S // 16], U16, name="offs_sb")
+        pos1_sb = held.tile([P, T // 16], U16, name="pos1_sb")
+        pos2_sb = held.tile([P, T // 16], U16, name="pos2_sb")
+        gate_sb = held.tile([P, S], F32, name="gate_sb")
+        wins = [[held.tile([P, WIN], F32, name=f"win{c}_{j}") for j in range(PACK)] for c in range(NPASS)]
+        wcodes = [[held.tile([P, K], U32, name=f"wcodes{e}_{c}", align_bytes=64) for c in range(NPASS)] for e in range(E)]
+        wscales = [[held.tile([P, K], U8, name=f"wscales{e}_{c}", align_bytes=64) for c in range(NPASS)] for e in range(E)]
+        gcodes = [[held.tile([P, HALF], U32, name=f"gcodes{c}_{h}", align_bytes=64) for h in range(2)] for c in range(NPASS)]
+        gscales = [[held.tile([P, HALF], U8, name=f"gscales{c}_{h}", align_bytes=64) for h in range(2)] for c in range(NPASS)]
+
+        for c in range(NPASS):
+            for j in range(PACK):
+                nc.gpsimd.memset(wins[c][j][:, T:WIN], 0.0)
+
+        def load_win(c, j):
+            rows = dyT[c * PASS : (c + 1) * PASS, :].rearrange("(p j) t -> p j t", j=PACK)
+            nc.sync.dma_start(wins[c][j][:, 0:T], rows[:, j, :])
+
+        def load_gate(h):
+            nc.sync.dma_start(gate_sb[:, h * HALF : (h + 1) * HALF], gate[0:P, h * HALF : (h + 1) * HALF])
+
+        wlist = [(e, c) for e in range(E) for c in range(NPASS)]
+        wraw = {}
+
+        def load_w(i, parts=1):
+            e, c = wlist[i]
+            raw = wraws.tile([P, PACK, K], F32, name="wraw")
+            wraw[i] = raw
+            rows = w[e, c * PASS : (c + 1) * PASS, :].rearrange("(p j) k -> p j k", j=PACK)
+            step = K // parts
+            for q in range(parts):
+                nc.sync.dma_start(raw[:, :, q * step : (q + 1) * step], rows[:, :, q * step : (q + 1) * step])
+
+        nc.sync.dma_start(offs_sb[:], offs)
+        load_win(0, 0)
+        load_gate(0)
+        load_win(0, 1)
+        load_w(0, 2)
+        load_win(0, 2)
+        load_win(0, 3)
+        load_gate(1)
+        load_w(1)
+        load_w(2)
+        load_win(1, 0)
+        load_win(1, 1)
+        load_win(1, 2)
+        load_win(1, 3)
+        load_w(3)
+        load_w(4)
+        load_win(2, 0)
+        load_win(2, 1)
+        load_win(2, 2)
+        load_win(2, 3)
+        for i in range(5, 12):
+            load_w(i)
+        nc.sync.dma_start(pos1_sb[:], pos1)
+        nc.sync.dma_start(pos2_sb[:], pos2)
+
+        def interleave(engine_copy, dst, src):
+            engine_copy(
+                dst.rearrange("p (c i t) -> p c t i", i=4, t=PACK),
+                src.rearrange("p t (c i) -> p c t i", i=4),
+            )
+
+        def do_g(c, h):
+            gf = gs.tile([P, PACK, HALF], F32, name="gf")
+            lists = offs_sb[:, h * 32 : (h + 1) * 32]
+            for j in range(PACK):
+                nc.vector.tensor_tensor(gf[:, j, :], wins[c][j][:].indirect(lists), gate_sb[:, h * HALF : (h + 1) * HALF], MULT)
+            gb = gs.tile([P, PACK * HALF], BF16, name="gb", align_bytes=64)
+            interleave(nc.scalar.copy, gb[:], gf[:])
+            nc.vector.quantize_mx(out=gcodes[c][h][:].bitcast(FP8X4), scales=gscales[c][h][:], in_=gb[:])
+
+        def do_w(i, half, copy):
+            e, c = wlist[i]
+            cols = slice(half * COLS, (half + 1) * COLS)
+            wb = wbfs.tile([P, PACK * COLS], BF16, name="wb", align_bytes=64)
+            interleave(copy, wb[:], wraw[i][:, :, cols])
+            nc.vector.quantize_mx(out=wcodes[e][c][:, cols].bitcast(FP8X4), scales=wscales[e][c][:, cols], in_=wb[:])
+
+        dxs = {}
+
+        def do_mm(kt):
+            dx = gs.tile([P, S], F32, name="dx")
+            dxs[kt] = dx
+            kcols = slice(kt * P, (kt + 1) * P)
+            for h in range(2):
+                acc = psum.tile([P, HALF], F32, name="acc")
+                for u in range(2):
+                    e = 2 * h + u
+                    scols = slice(u * C, (u + 1) * C)
+                    for c in range(NPASS):
+                        nc.tensor.matmul_mx(
+                            out=acc[:, scols],
+                            lhsT=wcodes[e][c][:, kcols].bitcast(FP8X4),
+                            lhsT_scale=wscales[e][c][:, kcols],
+                            rhs=gcodes[c][h][:, scols].bitcast(FP8X4),
+                            rhs_scale=gscales[c][h][:, scols],
+                            start=(c == 0),
+                            stop=(c == NPASS - 1),
+                        )
+                nc.scalar.copy(dx[:, h * HALF : (h + 1) * HALF], acc[:])
+
+        def do_out(kt):
+            r1 = gs.tile([P, T], F32, name="r1")
+            r2 = gs.tile([P, T], F32, name="r2")
+            nc.vector.tensor_copy(r1[:], dxs[kt][:].indirect(pos1_sb[:]))
+            nc.vector.tensor_copy(r2[:], dxs[kt][:].indirect(pos2_sb[:]))
+            res = gs.tile([P, T], F32, name="res")
+            nc.vector.tensor_tensor(res[:], r1[:], r2[:], ADD)
+            nc.sync.dma_start(out[kt * P : (kt + 1) * P, :], res[:])
+
+        done = 0
+        for c in range(NPASS):
+            for h in range(2):
+                do_g(c, h)
+                stop = (0, 1, 3, 5, 7, 8)[2 * c + h]
+                while done < stop:
+                    do_w(done, 0, nc.scalar.copy)
+                    done += 1
+        for i in range(done, 12):
+            do_w(i, 0, nc.scalar.copy)
+        do_mm(0)
+        do_mm(1)
+        for i in range(12):
+            do_w(i, 1, nc.vector.tensor_copy if i in VECTOR_B else nc.scalar.copy)
+        do_out(0)
+        do_out(1)
+        do_mm(2)
+        do_mm(3)
+        do_out(2)
+        do_out(3)

@@ -9,7 +9,6 @@ PACK = 4
 PASS = P * PACK
 NPASS = N // PASS
 HALF = 512
-WIN = T + 8
 COLS = 256
 
 F32 = mybir.dt.float32
@@ -24,15 +23,16 @@ MULT = mybir.AluOpType.mult
 FLOPS = 2 * K * N * S
 BYTES = 4 * (N * T + E * N * K + S + K * T) + 2 * 128 * (64 + 32 + 32)
 
-VECTOR_B = (10, 11)
+UNITS = ((0, 0, 1), (0, 1, 1), (1, 0, 2), (2, 0, 1), (2, 1, 1))
+NFULL = 6
 
 
 def tile_moe_bdx_lin_none_kernel(tc, dyT, w, gate, offs, pos1, pos2, out):
     nc = tc.nc
     with ExitStack() as ctx:
         held = ctx.enter_context(tc.tile_pool(name="held", bufs=1))
-        wraws = ctx.enter_context(tc.tile_pool(name="wraws", bufs=12))
-        wbfs = ctx.enter_context(tc.tile_pool(name="wbfs", bufs=12))
+        wraws = ctx.enter_context(tc.tile_pool(name="wraws", bufs=8))
+        wbfs = ctx.enter_context(tc.tile_pool(name="wbfs", bufs=4))
         gs = ctx.enter_context(tc.tile_pool(name="gs", bufs=2))
         psum = ctx.enter_context(tc.psum_pool(name="psum", bufs=8))
 
@@ -40,15 +40,15 @@ def tile_moe_bdx_lin_none_kernel(tc, dyT, w, gate, offs, pos1, pos2, out):
         pos1_sb = held.tile([P, T // 16], U16, name="pos1_sb")
         pos2_sb = held.tile([P, T // 16], U16, name="pos2_sb")
         gate_sb = held.tile([P, S], F32, name="gate_sb")
-        wins = [[held.tile([P, WIN], F32, name=f"win{c}_{j}") for j in range(PACK)] for c in range(NPASS)]
-        wcodes = [[held.tile([P, K], U32, name=f"wcodes{e}_{c}", align_bytes=64) for c in range(NPASS)] for e in range(E)]
-        wscales = [[held.tile([P, K], U8, name=f"wscales{e}_{c}", align_bytes=64) for c in range(NPASS)] for e in range(E)]
+        width = {c: n * HALF + 8 for c, h, n in UNITS}
+        wins = [[held.tile([P, width[c]], F32, name=f"win{c}_{j}") for j in range(PACK)] for c in range(NPASS)]
         gcodes = [[held.tile([P, HALF], U32, name=f"gcodes{c}_{h}", align_bytes=64) for h in range(2)] for c in range(NPASS)]
         gscales = [[held.tile([P, HALF], U8, name=f"gscales{c}_{h}", align_bytes=64) for h in range(2)] for c in range(NPASS)]
+        gf_wide = held.tile([P, PACK, S], F32, name="gf_wide")
 
         for c in range(NPASS):
             for j in range(PACK):
-                nc.gpsimd.memset(wins[c][j][:, T:WIN], 0.0)
+                nc.gpsimd.memset(wins[c][j][:, T : width[c]], 0.0)
 
         def load_win(c, j):
             rows = dyT[c * PASS : (c + 1) * PASS, :].rearrange("(p j) t -> p j t", j=PACK)
@@ -60,111 +60,206 @@ def tile_moe_bdx_lin_none_kernel(tc, dyT, w, gate, offs, pos1, pos2, out):
         wlist = [(e, c) for e in range(E) for c in range(NPASS)]
         wraw = {}
 
-        def load_w(i, parts=1):
+        def load_w(i, half=None):
             e, c = wlist[i]
-            raw = wraws.tile([P, PACK, K], F32, name="wraw")
-            wraw[i] = raw
+            if i not in wraw:
+                wraw[i] = wraws.tile([P, PACK, K], F32, name="wraw")
             rows = w[e, c * PASS : (c + 1) * PASS, :].rearrange("(p j) k -> p j k", j=PACK)
-            step = K // parts
-            for q in range(parts):
-                nc.sync.dma_start(raw[:, :, q * step : (q + 1) * step], rows[:, :, q * step : (q + 1) * step])
+            cols = slice(0, K) if half is None else slice(half * COLS, (half + 1) * COLS)
+            nc.sync.dma_start(wraw[i][:, :, cols], rows[:, :, cols])
 
-        nc.sync.dma_start(offs_sb[:], offs)
-        load_win(0, 0)
-        load_gate(0)
-        load_win(0, 1)
-        load_w(0, 2)
-        load_win(0, 2)
-        load_win(0, 3)
-        load_gate(1)
-        load_w(1)
-        load_w(2)
-        load_win(1, 0)
-        load_win(1, 1)
-        load_win(1, 2)
-        load_win(1, 3)
-        load_w(3)
-        load_w(4)
-        load_win(2, 0)
-        load_win(2, 1)
-        load_win(2, 2)
-        load_win(2, 3)
-        for i in range(5, 12):
-            load_w(i)
-        nc.sync.dma_start(pos1_sb[:], pos1)
-        nc.sync.dma_start(pos2_sb[:], pos2)
-
-        def interleave(engine_copy, dst, src):
-            engine_copy(
+        def interleave(copy, dst, src):
+            copy(
                 dst.rearrange("p (c i t) -> p c t i", i=4, t=PACK),
                 src.rearrange("p t (c i) -> p c t i", i=4),
             )
 
-        def do_g(c, h):
-            gf = gs.tile([P, PACK, HALF], F32, name="gf")
-            lists = offs_sb[:, h * 32 : (h + 1) * 32]
-            for j in range(PACK):
-                nc.vector.tensor_tensor(gf[:, j, :], wins[c][j][:].indirect(lists), gate_sb[:, h * HALF : (h + 1) * HALF], MULT)
-            gb = gs.tile([P, PACK * HALF], BF16, name="gb", align_bytes=64)
-            interleave(nc.scalar.copy, gb[:], gf[:])
-            nc.vector.quantize_mx(out=gcodes[c][h][:].bitcast(FP8X4), scales=gscales[c][h][:], in_=gb[:])
+        gfs, gbs, wbs, accs, dxs, rs, codes, scales = {}, {}, {}, {}, {}, {}, {}, {}
+        scopy, vcopy = nc.scalar.copy, nc.vector.tensor_copy
 
-        def do_w(i, half, copy):
-            e, c = wlist[i]
-            cols = slice(half * COLS, (half + 1) * COLS)
-            wb = wbfs.tile([P, PACK * COLS], BF16, name="wb", align_bytes=64)
-            interleave(copy, wb[:], wraw[i][:, :, cols])
-            nc.vector.quantize_mx(out=wcodes[e][c][:, cols].bitcast(FP8X4), scales=wscales[e][c][:, cols], in_=wb[:])
+        def G(u, j):
+            c, h, n = UNITS[u]
+            if j == 0:
+                gfs[u] = gf_wide if n == 2 else gs.tile([P, PACK, HALF], F32, name="gf")
+            lists = offs_sb[:, h * 32 : (h + n) * 32]
+            nc.vector.tensor_tensor(gfs[u][:, j, :], wins[c][j][:].indirect(lists), gate_sb[:, h * HALF : (h + n) * HALF], MULT)
 
-        dxs = {}
+        def GI(u, p=0):
+            gbs[u, p] = gs.tile([P, PACK * HALF], BF16, name="gb", align_bytes=64)
+            interleave(scopy, gbs[u, p][:], gfs[u][:, :, p * HALF : (p + 1) * HALF])
 
-        def do_mm(kt):
-            dx = gs.tile([P, S], F32, name="dx")
-            dxs[kt] = dx
-            kcols = slice(kt * P, (kt + 1) * P)
-            for h in range(2):
-                acc = psum.tile([P, HALF], F32, name="acc")
-                for u in range(2):
-                    e = 2 * h + u
-                    scols = slice(u * C, (u + 1) * C)
-                    for c in range(NPASS):
-                        nc.tensor.matmul_mx(
-                            out=acc[:, scols],
-                            lhsT=wcodes[e][c][:, kcols].bitcast(FP8X4),
-                            lhsT_scale=wscales[e][c][:, kcols],
-                            rhs=gcodes[c][h][:, scols].bitcast(FP8X4),
-                            rhs_scale=gscales[c][h][:, scols],
-                            start=(c == 0),
-                            stop=(c == NPASS - 1),
-                        )
-                nc.scalar.copy(dx[:, h * HALF : (h + 1) * HALF], acc[:])
+        def GQ(u, p=0):
+            c, h, n = UNITS[u]
+            nc.vector.quantize_mx(out=gcodes[c][h + p][:].bitcast(FP8X4), scales=gscales[c][h + p][:], in_=gbs[u, p][:])
 
-        def do_out(kt):
-            r1 = gs.tile([P, T], F32, name="r1")
-            r2 = gs.tile([P, T], F32, name="r2")
-            nc.vector.tensor_copy(r1[:], dxs[kt][:].indirect(pos1_sb[:]))
-            nc.vector.tensor_copy(r2[:], dxs[kt][:].indirect(pos2_sb[:]))
+        def new_wb(key):
+            wbs[key] = wbfs.tile([P, PACK * 2 * COLS], BF16, name="wb", align_bytes=64)
+            codes[key] = held.tile([P, 2 * COLS], U32, name=f"codes_{key}", align_bytes=64)
+            scales[key] = held.tile([P, 2 * COLS], U8, name=f"scales_{key}", align_bytes=64)
+
+        def F(i, copy=scopy, halves=False):
+            new_wb(f"F{i}")
+            wb = wbs[f"F{i}"]
+            if halves:
+                for h in range(2):
+                    interleave(copy, wb[:, h * PACK * COLS : (h + 1) * PACK * COLS], wraw[i][:, :, h * COLS : (h + 1) * COLS])
+            else:
+                interleave(copy, wb[:], wraw[i][:])
+
+        def AB(half, i, copy=scopy):
+            r = i % 2
+            key = f"{'AB'[half]}{i - r}"
+            if key not in wbs:
+                new_wb(key)
+            interleave(copy, wbs[key][:, r * PACK * COLS : (r + 1) * PACK * COLS], wraw[i][:, :, half * COLS : (half + 1) * COLS])
+
+        def WQ(key):
+            nc.vector.quantize_mx(out=codes[key][:].bitcast(FP8X4), scales=scales[key][:], in_=wbs[key][:])
+
+        def MM(kt, h):
+            acc = psum.tile([P, HALF], F32, name="acc")
+            accs[kt, h] = acc
+            for u in range(2):
+                scols = slice(u * C, (u + 1) * C)
+                for c in range(NPASS):
+                    i = (2 * h + u) * NPASS + c
+                    half, inner = divmod(kt, 2)
+                    if i < NFULL:
+                        key, k0 = f"F{i}", kt * P
+                    else:
+                        key, k0 = f"{'AB'[half]}{i - i % 2}", (i % 2) * COLS + inner * P
+                    nc.tensor.matmul_mx(
+                        out=acc[:, scols],
+                        lhsT=codes[key][:, k0 : k0 + P].bitcast(FP8X4),
+                        lhsT_scale=scales[key][:, k0 : k0 + P],
+                        rhs=gcodes[c][h][:, scols].bitcast(FP8X4),
+                        rhs_scale=gscales[c][h][:, scols],
+                        start=(c == 0),
+                        stop=(c == NPASS - 1),
+                    )
+
+        def PC(kt, h):
+            if kt not in dxs:
+                dxs[kt] = held.tile([P, S], F32, name=f"dx{kt}")
+            scopy(dxs[kt][:, h * HALF : (h + 1) * HALF], accs[kt, h][:])
+
+        def PO(kt, r):
+            rs[kt, r] = gs.tile([P, T], F32, name=f"r{r}")
+            vcopy(rs[kt, r][:], dxs[kt][:].indirect((pos1_sb, pos2_sb)[r][:]))
+
+        def AD(kt, engine):
             res = gs.tile([P, T], F32, name="res")
-            nc.vector.tensor_tensor(res[:], r1[:], r2[:], ADD)
+            engine.tensor_tensor(res[:], rs[kt, 0][:], rs[kt, 1][:], ADD)
             nc.sync.dma_start(out[kt * P : (kt + 1) * P, :], res[:])
 
-        done = 0
-        for c in range(NPASS):
-            for h in range(2):
-                do_g(c, h)
-                stop = (0, 1, 3, 5, 7, 8)[2 * c + h]
-                while done < stop:
-                    do_w(done, 0, nc.scalar.copy)
-                    done += 1
-        for i in range(done, 12):
-            do_w(i, 0, nc.scalar.copy)
-        do_mm(0)
-        do_mm(1)
-        for i in range(12):
-            do_w(i, 1, nc.vector.tensor_copy if i in VECTOR_B else nc.scalar.copy)
-        do_out(0)
-        do_out(1)
-        do_mm(2)
-        do_mm(3)
-        do_out(2)
-        do_out(3)
+        nc.sync.dma_start(offs_sb[:], offs)
+        load_win(0, 0)
+        load_gate(0)
+        load_w(0, 0)
+        load_win(0, 1)
+        load_win(0, 2)
+        load_w(0, 1)
+        load_win(0, 3)
+        load_w(1)
+        load_gate(1)
+        load_w(2)
+        for j in range(PACK):
+            load_win(1, j)
+        load_w(3)
+        load_w(4)
+        for j in range(PACK):
+            load_win(2, j)
+        load_w(5)
+        load_w(6)
+        nc.sync.dma_start(pos1_sb[:], pos1)
+        nc.sync.dma_start(pos2_sb[:], pos2)
+        for i in range(7, 12):
+            load_w(i)
+
+        G(0, 0)
+        G(0, 1)
+        F(0, halves=True)
+        G(0, 2)
+        G(0, 3)
+        GI(0)
+        WQ("F0")
+        G(1, 0)
+        G(1, 1)
+        F(1)
+        GQ(0)
+        G(1, 2)
+        F(2)
+        G(1, 3)
+        GI(1)
+        G(2, 0)
+        WQ("F1")
+        F(3)
+        G(2, 1)
+        GQ(1)
+        WQ("F2")
+        F(4)
+        G(2, 2)
+        F(5)
+        G(2, 3)
+        AB(0, 6)
+        WQ("F3")
+        GI(2, 0)
+        G(3, 0)
+        WQ("F4")
+        GI(2, 1)
+        G(3, 1)
+        AB(0, 7)
+        G(3, 2)
+        GQ(2, 0)
+        AB(0, 8)
+        G(3, 3)
+        GQ(2, 1)
+        GI(3)
+        G(4, 0)
+        WQ("F5")
+        AB(0, 9)
+        G(4, 1)
+        WQ("A6")
+        AB(0, 10)
+        G(4, 2)
+        AB(0, 11)
+        GQ(3)
+        G(4, 3)
+        GI(4)
+        WQ("A8")
+        for kt in range(4): MM(kt, 0)
+        AB(1, 10, vcopy)
+        WQ("A10")
+        AB(1, 11, vcopy)
+        AB(1, 6)
+        GQ(4)
+        WQ("B10")
+        AB(1, 7)
+        PC(0, 0)
+        PC(1, 0)
+        AB(1, 9, vcopy)
+        MM(0, 1)
+        MM(1, 1)
+        PC(0, 1)
+        WQ("B6")
+        PC(1, 1)
+        AB(1, 8)
+        PO(0, 0)
+        PO(0, 1)
+        WQ("B8")
+        PC(2, 0)
+        PC(3, 0)
+        PO(1, 0)
+        MM(2, 1)
+        MM(3, 1)
+        PC(2, 1)
+        PC(3, 1)
+        AD(0, nc.gpsimd)
+        PO(1, 1)
+        PO(2, 0)
+        AD(1, nc.gpsimd)
+        PO(2, 1)
+        PO(3, 0)
+        AD(2, nc.gpsimd)
+        PO(3, 1)
+        AD(3, nc.vector)

@@ -32,7 +32,7 @@ def tile_moe_bdx_lin_none_kernel(tc, dyT, w, gate, offs, pos1, pos2, out):
     with ExitStack() as ctx:
         held = ctx.enter_context(tc.tile_pool(name="held", bufs=1))
         wraws = ctx.enter_context(tc.tile_pool(name="wraws", bufs=8))
-        wbfs = ctx.enter_context(tc.tile_pool(name="wbfs", bufs=4))
+        wbfs = ctx.enter_context(tc.tile_pool(name="wbfs", bufs=6))
         gs = ctx.enter_context(tc.tile_pool(name="gs", bufs=2))
         psum = ctx.enter_context(tc.psum_pool(name="psum", bufs=8))
 
@@ -79,13 +79,13 @@ def tile_moe_bdx_lin_none_kernel(tc, dyT, w, gate, offs, pos1, pos2, out):
 
         def G(u, j):
             c, h, n = UNITS[u]
-            if j == 0:
+            if u not in gfs:
                 gfs[u] = gf_wide if n == 2 else gs.tile([P, PACK, HALF], F32, name="gf")
             lists = offs_sb[:, h * 32 : (h + n) * 32]
             nc.vector.tensor_tensor(gfs[u][:, j, :], wins[c][j][:].indirect(lists), gate_sb[:, h * HALF : (h + n) * HALF], MULT)
 
         def GI(u, p=0):
-            gbs[u, p] = gs.tile([P, PACK * HALF], BF16, name="gb", align_bytes=64)
+            gbs[u, p] = wbfs.tile([P, PACK * HALF], BF16, name="wb", align_bytes=64)
             interleave(scopy, gbs[u, p][:], gfs[u][:, :, p * HALF : (p + 1) * HALF])
 
         def GQ(u, p=0):
@@ -116,27 +116,27 @@ def tile_moe_bdx_lin_none_kernel(tc, dyT, w, gate, offs, pos1, pos2, out):
         def WQ(key):
             nc.vector.quantize_mx(out=codes[key][:].bitcast(FP8X4), scales=scales[key][:], in_=wbs[key][:])
 
-        def MM(kt, h):
-            acc = psum.tile([P, HALF], F32, name="acc")
-            accs[kt, h] = acc
-            for u in range(2):
+        def MM(kt, h, lo=0, hi=6):
+            if lo == 0:
+                accs[kt, h] = psum.tile([P, HALF], F32, name="acc")
+            for p in range(lo, hi):
+                u, c = divmod(p, NPASS)
                 scols = slice(u * C, (u + 1) * C)
-                for c in range(NPASS):
-                    i = (2 * h + u) * NPASS + c
-                    half, inner = divmod(kt, 2)
-                    if i < NFULL:
-                        key, k0 = f"F{i}", kt * P
-                    else:
-                        key, k0 = f"{'AB'[half]}{i - i % 2}", (i % 2) * COLS + inner * P
-                    nc.tensor.matmul_mx(
-                        out=acc[:, scols],
-                        lhsT=codes[key][:, k0 : k0 + P].bitcast(FP8X4),
-                        lhsT_scale=scales[key][:, k0 : k0 + P],
-                        rhs=gcodes[c][h][:, scols].bitcast(FP8X4),
-                        rhs_scale=gscales[c][h][:, scols],
-                        start=(c == 0),
-                        stop=(c == NPASS - 1),
-                    )
+                i = 2 * h * NPASS + p
+                half, inner = divmod(kt, 2)
+                if i < NFULL:
+                    key, k0 = f"F{i}", kt * P
+                else:
+                    key, k0 = f"{'AB'[half]}{i - i % 2}", (i % 2) * COLS + inner * P
+                nc.tensor.matmul_mx(
+                    out=accs[kt, h][:, scols],
+                    lhsT=codes[key][:, k0 : k0 + P].bitcast(FP8X4),
+                    lhsT_scale=scales[key][:, k0 : k0 + P],
+                    rhs=gcodes[c][h][:, scols].bitcast(FP8X4),
+                    rhs_scale=gscales[c][h][:, scols],
+                    start=(c == 0),
+                    stop=(c == NPASS - 1),
+                )
 
         def PC(kt, h):
             if kt not in dxs:
@@ -155,107 +155,110 @@ def tile_moe_bdx_lin_none_kernel(tc, dyT, w, gate, offs, pos1, pos2, out):
         nc.sync.dma_start(offs_sb[:], offs)
         load_win(0, 0)
         load_gate(0)
-        load_w(0, 0)
         load_win(0, 1)
+        load_w(0, 0)
         load_win(0, 2)
+        load_gate(1)
         load_w(0, 1)
         load_win(0, 3)
         load_w(1)
-        load_gate(1)
+        load_win(1, 0)
         load_w(2)
-        for j in range(PACK):
-            load_win(1, j)
+        load_win(1, 1)
         load_w(3)
+        load_win(1, 2)
         load_w(4)
-        for j in range(PACK):
-            load_win(2, j)
+        load_win(1, 3)
         load_w(5)
+        load_win(2, 0)
         load_w(6)
+        load_win(2, 1)
+        load_w(7)
+        load_win(2, 2)
+        load_win(2, 3)
         nc.sync.dma_start(pos1_sb[:], pos1)
         nc.sync.dma_start(pos2_sb[:], pos2)
-        for i in range(7, 12):
-            load_w(i)
-
+        for i in range(8, 12): load_w(i)
         G(0, 0)
         G(0, 1)
         F(0, halves=True)
         G(0, 2)
         G(0, 3)
-        GI(0)
-        WQ("F0")
+        F(1)
         G(1, 0)
         G(1, 1)
-        F(1)
-        GQ(0)
-        G(1, 2)
         F(2)
+        G(1, 2)
         G(1, 3)
-        GI(1)
+        F(3)
+        WQ("F0")
         G(2, 0)
         WQ("F1")
-        F(3)
-        G(2, 1)
-        GQ(1)
-        WQ("F2")
         F(4)
-        G(2, 2)
+        GI(0)
+        G(2, 1)
+        WQ("F2")
         F(5)
-        G(2, 3)
-        AB(0, 6)
+        G(2, 2)
         WQ("F3")
-        GI(2, 0)
-        G(3, 0)
+        GI(1)
+        G(2, 3)
         WQ("F4")
-        GI(2, 1)
+        GQ(0)
+        G(3, 0)
+        WQ("F5")
+        GI(2, 0)
         G(3, 1)
-        AB(0, 7)
+        GQ(1)
+        AB(0, 6)
+        GI(2, 1)
         G(3, 2)
+        AB(0, 7)
+        G(3, 3)
+        G(4, 0)
         GQ(2, 0)
         AB(0, 8)
-        G(3, 3)
-        GQ(2, 1)
-        GI(3)
-        G(4, 0)
-        WQ("F5")
-        AB(0, 9)
         G(4, 1)
-        WQ("A6")
-        AB(0, 10)
+        AB(0, 9)
+        GI(3)
+        GQ(2, 1)
         G(4, 2)
+        AB(0, 10)
         AB(0, 11)
-        GQ(3)
+        WQ("A6")
         G(4, 3)
         GI(4)
+        GQ(3)
         WQ("A8")
+        WQ("A10")
         for kt in range(4): MM(kt, 0)
         AB(1, 10, vcopy)
-        WQ("A10")
-        AB(1, 11, vcopy)
-        AB(1, 6)
-        GQ(4)
-        WQ("B10")
-        AB(1, 7)
+        AB(1, 11)
         PC(0, 0)
+        AB(1, 6, vcopy)
+        GQ(4)
+        AB(1, 7)
         PC(1, 0)
-        AB(1, 9, vcopy)
+        WQ("B10")
         MM(0, 1)
-        MM(1, 1)
-        PC(0, 1)
         WQ("B6")
-        PC(1, 1)
+        PC(0, 1)
+        MM(1, 1)
         AB(1, 8)
+        PC(1, 1)
+        AB(1, 9)
         PO(0, 0)
         PO(0, 1)
-        WQ("B8")
+        PO(1, 0)
+        PO(1, 1)
         PC(2, 0)
         PC(3, 0)
-        PO(1, 0)
+        WQ("B8")
         MM(2, 1)
         MM(3, 1)
         PC(2, 1)
         PC(3, 1)
         AD(0, nc.gpsimd)
-        PO(1, 1)
         PO(2, 0)
         AD(1, nc.gpsimd)
         PO(2, 1)

@@ -23,7 +23,7 @@ MULT = mybir.AluOpType.mult
 FLOPS = 2 * K * N * S
 BYTES = 4 * (N * T + E * N * K + S + K * T) + 2 * 128 * (64 + 32 + 32)
 
-UNITS = ((0, 0, 1), (0, 1, 1), (1, 0, 2), (2, 0, 1), (2, 1, 1))
+UNITS = ((0, 0, 2), (1, 0, 2), (2, 0, 2))
 NFULL = 6
 
 
@@ -31,7 +31,7 @@ def tile_moe_bdx_lin_none_kernel(tc, dyT, w, gate, offs, pos1, pos2, out):
     nc = tc.nc
     with ExitStack() as ctx:
         held = ctx.enter_context(tc.tile_pool(name="held", bufs=1))
-        wraws = ctx.enter_context(tc.tile_pool(name="wraws", bufs=8))
+        wraws = ctx.enter_context(tc.tile_pool(name="wraws", bufs=7))
         wbfs = ctx.enter_context(tc.tile_pool(name="wbfs", bufs=6))
         gs = ctx.enter_context(tc.tile_pool(name="gs", bufs=2))
         psum = ctx.enter_context(tc.psum_pool(name="psum", bufs=8))
@@ -40,19 +40,15 @@ def tile_moe_bdx_lin_none_kernel(tc, dyT, w, gate, offs, pos1, pos2, out):
         pos1_sb = held.tile([P, T // 16], U16, name="pos1_sb")
         pos2_sb = held.tile([P, T // 16], U16, name="pos2_sb")
         gate_sb = held.tile([P, S], F32, name="gate_sb")
-        width = {c: n * HALF + 8 for c, h, n in UNITS}
-        wins = [[held.tile([P, width[c]], F32, name=f"win{c}_{j}") for j in range(PACK)] for c in range(NPASS)]
         gcodes = [[held.tile([P, HALF], U32, name=f"gcodes{c}_{h}", align_bytes=64) for h in range(2)] for c in range(NPASS)]
         gscales = [[held.tile([P, HALF], U8, name=f"gscales{c}_{h}", align_bytes=64) for h in range(2)] for c in range(NPASS)]
-        gf_wide = held.tile([P, PACK, S], F32, name="gf_wide")
-
-        for c in range(NPASS):
-            for j in range(PACK):
-                nc.gpsimd.memset(wins[c][j][:, T : width[c]], 0.0)
+        wins = {}
 
         def load_win(c, j):
+            wins[c, j] = gs.tile([P, S + 8], F32, name=f"win{j}")
+            nc.gpsimd.memset(wins[c, j][:, T : S + 8], 0.0)
             rows = dyT[c * PASS : (c + 1) * PASS, :].rearrange("(p j) t -> p j t", j=PACK)
-            nc.sync.dma_start(wins[c][j][:, 0:T], rows[:, j, :])
+            nc.sync.dma_start(wins[c, j][:, 0:T], rows[:, j, :])
 
         def load_gate(h):
             nc.sync.dma_start(gate_sb[:, h * HALF : (h + 1) * HALF], gate[0:P, h * HALF : (h + 1) * HALF])
@@ -77,12 +73,11 @@ def tile_moe_bdx_lin_none_kernel(tc, dyT, w, gate, offs, pos1, pos2, out):
         gfs, gbs, wbs, accs, dxs, rs, codes, scales = {}, {}, {}, {}, {}, {}, {}, {}
         scopy, vcopy = nc.scalar.copy, nc.vector.tensor_copy
 
-        def G(u, j):
-            c, h, n = UNITS[u]
+        def G(u, j, h=None):
             if u not in gfs:
-                gfs[u] = gf_wide if n == 2 else gs.tile([P, PACK, HALF], F32, name="gf")
-            lists = offs_sb[:, h * 32 : (h + n) * 32]
-            nc.vector.tensor_tensor(gfs[u][:, j, :], wins[c][j][:].indirect(lists), gate_sb[:, h * HALF : (h + n) * HALF], MULT)
+                gfs[u] = gs.tile([P, PACK, S], F32, name="gf")
+            lo, hi = (0, S) if h is None else (h * HALF, (h + 1) * HALF)
+            nc.vector.tensor_tensor(gfs[u][:, j, lo:hi], wins[u, j][:].indirect(offs_sb[:, lo // 16 : hi // 16]), gate_sb[:, lo:hi], MULT)
 
         def GI(u, p=0):
             gbs[u, p] = wbfs.tile([P, PACK * HALF], BF16, name="wb", align_bytes=64)
@@ -155,10 +150,10 @@ def tile_moe_bdx_lin_none_kernel(tc, dyT, w, gate, offs, pos1, pos2, out):
         nc.sync.dma_start(offs_sb[:], offs)
         load_win(0, 0)
         load_gate(0)
+        load_gate(1)
         load_win(0, 1)
         load_w(0, 0)
         load_win(0, 2)
-        load_gate(1)
         load_w(0, 1)
         load_win(0, 3)
         load_w(1)
@@ -170,94 +165,88 @@ def tile_moe_bdx_lin_none_kernel(tc, dyT, w, gate, offs, pos1, pos2, out):
         load_w(4)
         load_win(1, 3)
         load_w(5)
+        nc.sync.dma_start(pos1_sb[:], pos1)
+        nc.sync.dma_start(pos2_sb[:], pos2)
         load_win(2, 0)
         load_w(6)
         load_win(2, 1)
         load_w(7)
         load_win(2, 2)
+        load_w(8)
         load_win(2, 3)
-        nc.sync.dma_start(pos1_sb[:], pos1)
-        nc.sync.dma_start(pos2_sb[:], pos2)
-        for i in range(8, 12): load_w(i)
-        G(0, 0)
+        for i in range(9, 12): load_w(i)
+        G(0, 0, 0)
+        G(0, 0, 1)
         G(0, 1)
         F(0, halves=True)
+        F(1)
         G(0, 2)
         G(0, 3)
-        F(1)
-        G(1, 0)
-        G(1, 1)
+        GI(0, 0)
         F(2)
-        G(1, 2)
-        G(1, 3)
         F(3)
+        G(1, 0)
         WQ("F0")
-        G(2, 0)
-        WQ("F1")
         F(4)
-        GI(0)
-        G(2, 1)
-        WQ("F2")
+        G(1, 1)
+        WQ("F1")
         F(5)
-        G(2, 2)
+        G(1, 2)
+        GQ(0, 0)
+        WQ("F2")
+        GI(0, 1)
+        G(1, 3)
         WQ("F3")
-        GI(1)
-        G(2, 3)
-        WQ("F4")
-        GQ(0)
-        G(3, 0)
-        WQ("F5")
-        GI(2, 0)
-        G(3, 1)
-        GQ(1)
         AB(0, 6)
-        GI(2, 1)
-        G(3, 2)
         AB(0, 7)
-        G(3, 3)
-        G(4, 0)
-        GQ(2, 0)
+        G(2, 0)
+        WQ("F4")
+        GI(1, 0)
+        GI(1, 1)
+        G(2, 1)
+        WQ("F5")
+        GQ(0, 1)
         AB(0, 8)
-        G(4, 1)
         AB(0, 9)
-        GI(3)
-        GQ(2, 1)
-        G(4, 2)
+        G(2, 2)
+        WQ("A6")
+        GQ(1, 0)
         AB(0, 10)
         AB(0, 11)
-        WQ("A6")
-        G(4, 3)
-        GI(4)
-        GQ(3)
+        G(2, 3)
+        GQ(1, 1)
+        GI(2, 0)
         WQ("A8")
         WQ("A10")
+        GI(2, 1)
+        GQ(2, 0)
         for kt in range(4): MM(kt, 0)
         AB(1, 10, vcopy)
-        AB(1, 11)
-        PC(0, 0)
-        AB(1, 6, vcopy)
-        GQ(4)
-        AB(1, 7)
-        PC(1, 0)
-        WQ("B10")
-        MM(0, 1)
-        WQ("B6")
-        PC(0, 1)
-        MM(1, 1)
+        AB(1, 11, vcopy)
         AB(1, 8)
-        PC(1, 1)
+        AB(1, 6, vcopy)
+        PC(0, 0)
+        GQ(2, 1)
         AB(1, 9)
+        WQ("B10")
+        AB(1, 7, vcopy)
+        WQ("B6")
+        MM(0, 1)
+        MM(1, 1)
+        PC(1, 0)
+        PC(0, 1)
+        PC(1, 1)
+        WQ("B8")
         PO(0, 0)
         PO(0, 1)
-        PO(1, 0)
-        PO(1, 1)
-        PC(2, 0)
-        PC(3, 0)
-        WQ("B8")
         MM(2, 1)
         MM(3, 1)
+        PC(2, 0)
+        PC(3, 0)
+        PO(1, 0)
         PC(2, 1)
         PC(3, 1)
+        PO(1, 1)
         AD(0, nc.gpsimd)
         PO(2, 0)
         AD(1, nc.gpsimd)

from contextlib import ExitStack

import concourse.mybir as mybir

K, T, E, C, N = 512, 512, 4, 256, 1536
S = E * C
P = 128
PACK = 4
PASS = P * PACK
NPASS = N // PASS
HALF = 512
COLS = 256

F32 = mybir.dt.float32
BF16 = mybir.dt.bfloat16
U32 = mybir.dt.uint32
U16 = mybir.dt.uint16
U8 = mybir.dt.uint8
FP8X4 = mybir.dt.float8_e4m3fn_x4
ADD = mybir.AluOpType.add
MULT = mybir.AluOpType.mult

FLOPS = 2 * K * N * S
BYTES = 4 * (N * T + E * N * K + S + K * T) + 2 * 128 * (64 + 32 + 32)

UNITS = ((0, 0, 2), (1, 0, 2), (2, 0, 2))
NFULL = 6


def tile_moe_bdx_lin_none_kernel(tc, dyT, w, gate, offs, pos1, pos2, out):
    nc = tc.nc
    with ExitStack() as ctx:
        held = ctx.enter_context(tc.tile_pool(name="held", bufs=1))
        wraws = ctx.enter_context(tc.tile_pool(name="wraws", bufs=7))
        wbfs = ctx.enter_context(tc.tile_pool(name="wbfs", bufs=6))
        gs = ctx.enter_context(tc.tile_pool(name="gs", bufs=2))
        psum = ctx.enter_context(tc.psum_pool(name="psum", bufs=8))

        offs_sb = held.tile([P, S // 16], U16, name="offs_sb")
        pos1_sb = held.tile([P, T // 16], U16, name="pos1_sb")
        pos2_sb = held.tile([P, T // 16], U16, name="pos2_sb")
        gate_sb = held.tile([P, S], F32, name="gate_sb")
        gcodes = [[held.tile([P, HALF], U32, name=f"gcodes{c}_{h}", align_bytes=64) for h in range(2)] for c in range(NPASS)]
        gscales = [[held.tile([P, HALF], U8, name=f"gscales{c}_{h}", align_bytes=64) for h in range(2)] for c in range(NPASS)]
        wins = {}

        def load_win(c, j):
            wins[c, j] = gs.tile([P, S + 8], F32, name=f"win{j}")
            nc.gpsimd.memset(wins[c, j][:, T : S + 8], 0.0)
            rows = dyT[c * PASS : (c + 1) * PASS, :].rearrange("(p j) t -> p j t", j=PACK)
            nc.sync.dma_start(wins[c, j][:, 0:T], rows[:, j, :])

        def load_gate(h):
            nc.sync.dma_start(gate_sb[:, h * HALF : (h + 1) * HALF], gate[0:P, h * HALF : (h + 1) * HALF])

        wlist = [(e, c) for e in range(E) for c in range(NPASS)]
        wraw = {}

        def load_w(i, half=None):
            e, c = wlist[i]
            if i not in wraw:
                wraw[i] = wraws.tile([P, PACK, K], F32, name="wraw")
            rows = w[e, c * PASS : (c + 1) * PASS, :].rearrange("(p j) k -> p j k", j=PACK)
            cols = slice(0, K) if half is None else slice(half * COLS, (half + 1) * COLS)
            nc.sync.dma_start(wraw[i][:, :, cols], rows[:, :, cols])

        def interleave(copy, dst, src):
            copy(
                dst.rearrange("p (c i t) -> p c t i", i=4, t=PACK),
                src.rearrange("p t (c i) -> p c t i", i=4),
            )

        gfs, gbs, wbs, accs, dxs, rs, codes, scales = {}, {}, {}, {}, {}, {}, {}, {}
        scopy, vcopy = nc.scalar.copy, nc.vector.tensor_copy

        def G(u, j, h=None):
            if u not in gfs:
                gfs[u] = gs.tile([P, PACK, S], F32, name="gf")
            lo, hi = (0, S) if h is None else (h * HALF, (h + 1) * HALF)
            nc.vector.tensor_tensor(gfs[u][:, j, lo:hi], wins[u, j][:].indirect(offs_sb[:, lo // 16 : hi // 16]), gate_sb[:, lo:hi], MULT)

        def GI(u, p=0):
            gbs[u, p] = wbfs.tile([P, PACK * HALF], BF16, name="wb", align_bytes=64)
            interleave(scopy, gbs[u, p][:], gfs[u][:, :, p * HALF : (p + 1) * HALF])

        def GQ(u, p=0):
            c, h, n = UNITS[u]
            nc.vector.quantize_mx(out=gcodes[c][h + p][:].bitcast(FP8X4), scales=gscales[c][h + p][:], in_=gbs[u, p][:])

        def new_wb(key):
            wbs[key] = wbfs.tile([P, PACK * 2 * COLS], BF16, name="wb", align_bytes=64)
            codes[key] = held.tile([P, 2 * COLS], U32, name=f"codes_{key}", align_bytes=64)
            scales[key] = held.tile([P, 2 * COLS], U8, name=f"scales_{key}", align_bytes=64)

        def F(i, copy=scopy, halves=False):
            new_wb(f"F{i}")
            wb = wbs[f"F{i}"]
            if halves:
                for h in range(2):
                    interleave(copy, wb[:, h * PACK * COLS : (h + 1) * PACK * COLS], wraw[i][:, :, h * COLS : (h + 1) * COLS])
            else:
                interleave(copy, wb[:], wraw[i][:])

        def AB(half, i, copy=scopy):
            r = i % 2
            key = f"{'AB'[half]}{i - r}"
            if key not in wbs:
                new_wb(key)
            interleave(copy, wbs[key][:, r * PACK * COLS : (r + 1) * PACK * COLS], wraw[i][:, :, half * COLS : (half + 1) * COLS])

        def WQ(key):
            nc.vector.quantize_mx(out=codes[key][:].bitcast(FP8X4), scales=scales[key][:], in_=wbs[key][:])

        def MM(kt, h, lo=0, hi=6):
            if lo == 0:
                accs[kt, h] = psum.tile([P, HALF], F32, name="acc")
            for p in range(lo, hi):
                u, c = divmod(p, NPASS)
                scols = slice(u * C, (u + 1) * C)
                i = 2 * h * NPASS + p
                half, inner = divmod(kt, 2)
                if i < NFULL:
                    key, k0 = f"F{i}", kt * P
                else:
                    key, k0 = f"{'AB'[half]}{i - i % 2}", (i % 2) * COLS + inner * P
                nc.tensor.matmul_mx(
                    out=accs[kt, h][:, scols],
                    lhsT=codes[key][:, k0 : k0 + P].bitcast(FP8X4),
                    lhsT_scale=scales[key][:, k0 : k0 + P],
                    rhs=gcodes[c][h][:, scols].bitcast(FP8X4),
                    rhs_scale=gscales[c][h][:, scols],
                    start=(c == 0),
                    stop=(c == NPASS - 1),
                )

        def PC(kt, h):
            if kt not in dxs:
                dxs[kt] = held.tile([P, S], F32, name=f"dx{kt}")
            scopy(dxs[kt][:, h * HALF : (h + 1) * HALF], accs[kt, h][:])

        def PO(kt, r):
            rs[kt, r] = gs.tile([P, T], F32, name=f"r{r}")
            vcopy(rs[kt, r][:], dxs[kt][:].indirect((pos1_sb, pos2_sb)[r][:]))

        def AD(kt, engine):
            res = gs.tile([P, T], F32, name="res")
            engine.tensor_tensor(res[:], rs[kt, 0][:], rs[kt, 1][:], ADD)
            nc.sync.dma_start(out[kt * P : (kt + 1) * P, :], res[:])

        nc.sync.dma_start(offs_sb[:], offs)
        load_win(0, 0)
        load_gate(0)
        load_gate(1)
        load_win(0, 1)
        load_w(0, 0)
        load_win(0, 2)
        load_w(0, 1)
        load_win(0, 3)
        load_w(1)
        load_win(1, 0)
        load_w(2)
        load_win(1, 1)
        load_w(3)
        load_win(1, 2)
        load_w(4)
        load_win(1, 3)
        load_w(5)
        nc.sync.dma_start(pos1_sb[:], pos1)
        nc.sync.dma_start(pos2_sb[:], pos2)
        load_win(2, 0)
        load_w(6)
        load_win(2, 1)
        load_w(7)
        load_win(2, 2)
        load_w(8)
        load_win(2, 3)
        for i in range(9, 12): load_w(i)
        G(0, 0, 0)
        G(0, 0, 1)
        G(0, 1)
        F(0, halves=True)
        F(1)
        G(0, 2)
        G(0, 3)
        GI(0, 0)
        F(2)
        F(3)
        G(1, 0)
        WQ("F0")
        F(4)
        G(1, 1)
        WQ("F1")
        F(5)
        G(1, 2)
        GQ(0, 0)
        WQ("F2")
        GI(0, 1)
        G(1, 3)
        WQ("F3")
        AB(0, 6)
        AB(0, 7)
        G(2, 0)
        WQ("F4")
        GI(1, 0)
        GI(1, 1)
        G(2, 1)
        WQ("F5")
        GQ(0, 1)
        AB(0, 8)
        AB(0, 9)
        G(2, 2)
        WQ("A6")
        GQ(1, 0)
        AB(0, 10)
        AB(0, 11)
        G(2, 3)
        GQ(1, 1)
        GI(2, 0)
        WQ("A8")
        WQ("A10")
        GI(2, 1)
        GQ(2, 0)
        for kt in range(4): MM(kt, 0)
        AB(1, 10, vcopy)
        AB(1, 11, vcopy)
        AB(1, 8)
        AB(1, 6, vcopy)
        PC(0, 0)
        GQ(2, 1)
        AB(1, 9)
        WQ("B10")
        AB(1, 7, vcopy)
        WQ("B6")
        MM(0, 1)
        MM(1, 1)
        PC(1, 0)
        PC(0, 1)
        PC(1, 1)
        WQ("B8")
        PO(0, 0)
        PO(0, 1)
        MM(2, 1)
        MM(3, 1)
        PC(2, 0)
        PC(3, 0)
        PO(1, 0)
        PC(2, 1)
        PC(3, 1)
        PO(1, 1)
        AD(0, nc.gpsimd)
        PO(2, 0)
        AD(1, nc.gpsimd)
        PO(2, 1)
        PO(3, 0)
        AD(2, nc.gpsimd)
        PO(3, 1)
        AD(3, nc.vector)
